import numpy as np
import ml_dtypes


def mxq(x, axis, fmt="e4m3"):
    dtype, down = {"e4m3": (ml_dtypes.float8_e4m3fn, 7), "e5m2": (ml_dtypes.float8_e5m2, 14)}[fmt]
    v = np.moveaxis(np.asarray(x, np.float32).astype(ml_dtypes.bfloat16).astype(np.float64), axis, -1)
    blocks = v.reshape(v.shape[:-1] + (-1, 32))
    amax = np.abs(blocks).max(-1, keepdims=True)
    byte = np.maximum(np.where(amax > 0, np.frexp(amax)[1] - 1 + 127, 0) - down, 1)
    scale = np.exp2(byte - 127.0)
    codes = (blocks / scale).astype(np.float32).astype(dtype).astype(np.float64)
    return np.moveaxis((codes * scale).reshape(v.shape), -1, axis)


WIDE = False


def mx_kscale(k):
    if not WIDE:
        return np.ones(k)
    levels = np.array([10, -10, 5, -5, 0])
    if k % 512:
        return np.exp2(np.random.permutation(np.resize(levels, k // 32))).repeat(32)
    a = np.empty((k // 512, 16))
    for p in range(k // 512):
        a[p, :8] = np.random.permutation(np.resize(levels, 8))
        for g in range(8):
            far = levels[np.abs(levels - a[p, g]) >= 10]
            a[p, g + 8] = far[np.random.randint(len(far))]
    return np.exp2(a.ravel()).repeat(32)


def f64(x):
    return np.asarray(x).astype(np.float64)


def striped(idx):
    return np.tile(idx.reshape(-1, 16).T, (8, 1)).astype(np.uint16)


def unstriped(offs):
    return offs[:16].T.reshape(-1).astype(np.int64)


E2M1 = np.array([0.0, 0.5, 1.0, 1.5, 2.0, 3.0, 4.0, 6.0, -0.0, -0.5, -1.0, -1.5, -2.0, -3.0, -4.0, -6.0])


def pack_weight(w, fmt):
    k, n = w.shape
    w = f64(np.asarray(w, np.float32).astype(ml_dtypes.bfloat16)).reshape(k // 32, 32, n)
    amax = np.abs(w).max(1)
    if fmt == "e4m3":
        byte = np.frexp(amax)[1] - 1 + 127 - 7
    else:
        mant, ex = np.frexp(amax / 6.0)
        byte = np.where(mant > 0.5, ex, ex - 1) + 127
    byte = np.clip(np.where(amax > 0, byte, 1), 1, 254)
    scaled = (w * np.exp2(127.0 - byte)[:, None, :]).reshape(k, n).astype(np.float32)
    by_word = np.ascontiguousarray(scaled.reshape(k // 512, 128, 4, n).transpose(0, 1, 3, 2))
    if fmt == "e4m3":
        words = by_word.astype(ml_dtypes.float8_e4m3fn).view(np.uint8)
    else:
        c = by_word.astype(ml_dtypes.float4_e2m1fn).view(np.uint8) & 0xF
        words = (c[..., 0::2] | (c[..., 1::2] << 4)).reshape(k // 512, 128, 2 * n)
    return np.ascontiguousarray(words), np.ascontiguousarray(byte.astype(np.uint8).reshape(k // 512, 16, n))


def unpack_weight(words, scales, fmt):
    g, _, n = scales.shape
    words = np.ascontiguousarray(words).reshape(g, 128, n, -1)
    if fmt == "e4m3":
        vals = words.view(ml_dtypes.float8_e4m3fn).astype(np.float64)
    else:
        nib = np.empty((g, 128, n, 4), np.uint8)
        nib[..., 0::2] = words & 0xF
        nib[..., 1::2] = words >> 4
        vals = E2M1[nib]
    vals = vals * np.repeat(np.exp2(scales.astype(np.float64) - 127.0), 8, axis=1)[..., None]
    return vals.transpose(0, 1, 3, 2).reshape(g * 512, n)


def gelu(v):
    return 0.5 * v * (1.0 + np.tanh(np.sqrt(2.0 / np.pi) * (v + 0.044715 * v**3)))


def often(T, S):
    return np.random.permutation(T)[(T * np.random.uniform(0, 1, S) ** 4).astype(np.int64)]


def bf(x):
    return np.asarray(x, np.float32).astype(ml_dtypes.bfloat16)


def planes(Y):
    n, m = Y.shape
    b = f64(bf(Y)).reshape(n // 32, 32, m)
    amax = np.abs(b).max(1)
    byte = np.clip(np.where(amax > 0, np.frexp(amax)[1] - 1 + 127 - 7, 1), 1, 254)
    codes = (b * np.exp2(127.0 - byte)[:, None, :]).reshape(n, m).astype(np.float32).astype(ml_dtypes.float8_e4m3fn).view(np.uint8)
    words = codes.reshape(n // 512, 128, 4, m).transpose(0, 1, 3, 2)
    return np.ascontiguousarray(words), np.ascontiguousarray(byte.astype(np.uint8).reshape(n // 512, 16, m))


K, K2, H, N, T, S, P = 1024, 512, 1024, 512, 4096, 1024, 512


def setup_inputs():
    n = np.random.standard_normal
    s, s2, u = mx_kscale(K)[:, None], mx_kscale(K2)[:, None], mx_kscale(H)[:, None]
    d = {}
    d["tab_words"], d["tab_scales"] = pack_weight(n((K, T)) * s, "e4m3")
    d["tab2_words"], d["tab2_scales"] = pack_weight(n((K2, T)) * s2, "e4m3")
    d["tab3_words"], d["tab3_scales"] = pack_weight(n((K2, T)) * s2, "e4m3")
    d["offs"] = striped(np.random.permutation(T)[:S])
    d["offs2"] = striped(np.random.permutation(T)[:S])
    d["offs3"] = striped(np.random.permutation(T)[:S])
    d["pos1"] = striped(np.random.permutation(S)[:P])
    d["pos2"] = striped(often(S, P))
    d["pos3"] = striped(often(S, P))
    d["w1"] = (n((K, H)) / K ** 0.5 / s * u.T).astype(np.float32)
    d["w2_words"], d["w2_scales"] = pack_weight(n((K2, H)) / K2 ** 0.5 / s2 * u.T, "e2m1")
    d["w3"] = (n((K2, H)) / K2 ** 0.5 / s2 * u.T).astype(np.float32)
    d["w4_words"], d["w4_scales"] = pack_weight(n((H, N)) / H ** 0.5 / u * np.exp(0.8 * n(N)), "e4m3")
    return d


def reference(tab_words, tab_scales, tab2_words, tab2_scales, tab3_words, tab3_scales,
              offs, offs2, offs3, pos1, pos2, pos3, w1, w2_words, w2_scales, w3, w4_words, w4_scales):
    v = unpack_weight(tab_words, tab_scales, "e4m3")[:, unstriped(offs)]
    v2 = unpack_weight(tab2_words, tab2_scales, "e4m3")[:, unstriped(offs2)]
    v3 = unpack_weight(tab3_words, tab3_scales, "e4m3")[:, unstriped(offs3)]
    a = mxq(f64(w1), 0, "e4m3").T @ v
    b = unpack_weight(w2_words, w2_scales, "e2m1").T @ v2
    d = mxq(f64(w3), 0, "e4m3").T @ v3
    bt = b[:, unstriped(pos2)]
    z = np.maximum(a[:, unstriped(pos1)] - bt, bt - d[:, unstriped(pos3)])
    y = unpack_weight(w4_words, w4_scales, "e4m3").T @ mxq(z, 0, "e4m3")
    words, scales = planes(y)
    return y, words, scales

@@ -1,0 +1,287 @@
+from contextlib import ExitStack
+
+import concourse.mybir as mybir
+
+K, K2, H, N, T, S, J = 1024, 512, 1024, 512, 4096, 1024, 512
+FLOPS = 2 * (K * H * S + 2 * K2 * H * S + H * N * J)
+
+F32 = mybir.dt.float32
+BF16 = mybir.dt.bfloat16
+I32 = mybir.dt.int32
+U32 = mybir.dt.uint32
+U16 = mybir.dt.uint16
+U8 = mybir.dt.uint8
+FP8X4 = mybir.dt.float8_e4m3fn_x4
+FP4X4 = mybir.dt.float4_e2m1fn_x4
+ALU = mybir.AluOpType
+COPY = mybir.ActivationFunctionType.Copy
+
+P = 128
+PACK = 4
+PASS = P * PACK
+BANK = 512
+QUARTER = 128
+
+
+def tile_list_milk_coldstep_features_kernel(
+    tc, tab_words, tab_scales, tab2_words, tab2_scales, tab3_words, tab3_scales,
+    offs, offs2, offs3, pos1, pos2, pos3, w1, w2_words, w2_scales, w3, w4_words, w4_scales,
+    out_0, out_1, out_2,
+):
+    nc = tc.nc
+    with ExitStack() as ctx:
+        keep = ctx.enter_context(tc.tile_pool(name="keep", bufs=1))
+        ring = ctx.enter_context(tc.tile_pool(name="ring", bufs=1))
+        psum = ctx.enter_context(tc.psum_pool(name="psum", bufs=1))
+
+        def load_list(dram, name):
+            tile = keep.tile(list(dram.shape), U16, name=name)
+            nc.sync.dma_start(tile[:], dram)
+            return tile
+
+        def zeroed_plane(width, name, engine):
+            tile = keep.tile([P, width], U8, name=name, align_bytes=64)
+            engine.memset(tile[:].bitcast(I32), 0)
+            return tile
+
+        def load_scale_rows(queue, plane, scales, first):
+            passes = scales.shape[0]
+            for quad in range(4):
+                rows = scales[:, 4 * quad : 4 * quad + 4, :] if passes > 1 else scales[0, 4 * quad : 4 * quad + 4, :]
+                queue.dma_start(
+                    out=plane[32 * quad + first : 32 * quad + first + 4 * passes, :].bitcast(I32),
+                    in_=rows.bitcast(I32),
+                )
+
+        def load_spread_rows(queue, window, scales):
+            rows = scales.rearrange("a q t -> (a q) t")
+            queue.dma_start(out=window[0 : P : P // rows.shape[0], :].bitcast(I32), in_=rows.bitcast(I32))
+
+        def place_rows(queue, picked, passes, name):
+            plane = zeroed_plane(S, name, nc.vector)
+            step = P // (16 * passes)
+            for a in range(passes):
+                for r in range(4):
+                    first = step * (16 * a + r)
+                    queue.dma_start(
+                        out=plane[4 * a + r : P : 32, :].bitcast(I32),
+                        in_=picked[first : first + 12 * step + 1 : 4 * step, :].bitcast(I32),
+                    )
+            return plane
+
+        def load_table_words(words, a):
+            tile = ring.tile([P, T], U32, name="table", tag="table", bufs=3)
+            nc.sync.dma_start(out=tile[:].bitcast(I32), in_=words[a].rearrange("p t i -> p (t i)").bitcast(I32))
+            return tile
+
+        def load_weight(w, a, b):
+            tile = ring.tile([P, PACK, PASS], F32, name="raw", tag="raw", bufs=4)
+            nc.sync.dma_start(
+                out=tile[:],
+                in_=w[PASS * a : PASS * (a + 1), PASS * b : PASS * (b + 1)].rearrange("(p i) c -> p i c", i=PACK),
+            )
+            return tile
+
+        def round_weight(raw):
+            rounded = ring.tile([P, PACK * PASS], BF16, name="rounded", tag="rounded", bufs=3, align_bytes=64)
+            nc.scalar.activation(
+                out=rounded[:].rearrange("p (t m i) -> p m i t", t=PACK, i=PACK),
+                in_=raw[:].rearrange("p i (m t) -> p m i t", t=PACK),
+                func=COPY,
+            )
+            return rounded
+
+        def quantize(rounded, name):
+            width = rounded.shape[1] // PACK
+            codes = keep.tile([P, width], U32, name=name + "_codes", align_bytes=64)
+            scales = keep.tile([P, width], U8, name=name + "_scales", align_bytes=64)
+            nc.vector.quantize_mx(out=codes[:].bitcast(FP8X4), scales=scales[:], in_=rounded)
+            return codes, scales
+
+        def gather(window, offsets, dtype, name):
+            picked = keep.tile([P, 16 * offsets.shape[1]], dtype, name=name, align_bytes=64)
+            nc.vector.tensor_copy(picked[:], window[:].indirect(offsets))
+            return picked
+
+        def first_stage_rows(passes, sign):
+            rows = ring.tile([P, S], F32, name="rows", tag="rows", bufs=6)
+            for half in range(S // BANK):
+                bank = psum.tile([P, BANK], F32, name="bank", tag="bank", bufs=4)
+                for a, (lhsT, lhsT_scale, moving, moving_scale) in enumerate(passes):
+                    nc.tensor.matmul_mx(
+                        out=bank[:], lhsT=lhsT, lhsT_scale=lhsT_scale, rhs=moving[half], rhs_scale=moving_scale[half],
+                        start=(a == 0), stop=(a == len(passes) - 1),
+                    )
+                cols = rows[:, BANK * half : BANK * (half + 1)]
+                if sign > 0:
+                    nc.scalar.copy(out=cols, in_=bank[:])
+                else:
+                    nc.scalar.activation(out=cols, in_=bank[:], func=COPY, scale=-1.0)
+            return rows
+
+        def halves(tile, first_row=0):
+            return [tile[first_row:P, BANK * h : BANK * (h + 1)] for h in range(S // BANK)]
+
+        s2_win = zeroed_plane(T, "s2_win", nc.vector)
+        s3_win = zeroed_plane(T, "s3_win", nc.vector)
+        w2s_raw = zeroed_plane(H, "w2s_raw", nc.vector)
+        s1_win = zeroed_plane(T, "s1_win", nc.vector)
+        w4s_raw = zeroed_plane(N, "w4s_raw", nc.vector)
+
+        o2 = load_list(offs2, "o2")
+        load_scale_rows(nc.sync, s2_win, tab2_scales, 0)
+        o3 = load_list(offs3, "o3")
+        w2_raw = keep.tile([P, H], U16, name="w2_raw")
+        nc.sync.dma_start(out=w2_raw[:].bitcast(I32), in_=w2_words[0].bitcast(I32))
+        p2 = load_list(pos2, "p2")
+        load_spread_rows(nc.sync, s3_win, tab3_scales)
+        o1 = load_list(offs, "o1")
+        t2_win = load_table_words(tab2_words, 0)
+        load_scale_rows(nc.sync, w2s_raw, w2_scales, 0)
+        load_spread_rows(nc.sync, s1_win, tab_scales)
+        w3_raw = [load_weight(w3, 0, b) for b in range(2)]
+        t3_win = load_table_words(tab3_words, 0)
+        p3 = load_list(pos3, "p3")
+        p1 = load_list(pos1, "p1")
+        w1_raw = {}
+        for b in range(2):
+            for a in range(2):
+                w1_raw[a, b] = load_weight(w1, a, b)
+        load_scale_rows(nc.sync, w4s_raw, w4_scales, 0)
+        w4_raw = keep.tile([P, 2, N], U32, name="w4_raw")
+        nc.sync.dma_start(out=w4_raw[:].bitcast(I32), in_=w4_words.rearrange("a p c i -> p a (c i)").bitcast(I32))
+        t1_win = [load_table_words(tab_words, a) for a in range(2)]
+
+        s2 = gather(s2_win, o2[:], U8, "s2")
+        s3 = place_rows(nc.gpsimd, gather(s3_win, o3[:], U8, "s3_picked"), 1, "s3")
+        w3_rounded = [round_weight(w3_raw[0])]
+        w2c = keep.tile([P, H], U16, name="w2c", align_bytes=64)
+        nc.scalar.copy(
+            out=w2c[:].rearrange("p (b t m) -> p b m t", b=2, t=PACK),
+            in_=w2_raw[:].rearrange("p (b m t) -> p b m t", b=2, t=PACK),
+        )
+        w2s = keep.tile([P, H], U8, name="w2s", align_bytes=64)
+        nc.vector.tensor_copy(
+            out=w2s[:].rearrange("p (b t m) -> p b m t", b=2, t=PACK),
+            in_=w2s_raw[:].rearrange("p (b m t) -> p b m t", b=2, t=PACK),
+        )
+        v2 = [gather(t2_win, o2[:, 32 * h : 32 * (h + 1)], U32, "v2_%d" % h) for h in range(2)]
+        s1 = place_rows(nc.gpsimd, gather(s1_win, o1[:], U8, "s1_picked"), 2, "s1")
+        w3q = [quantize(w3_rounded[0][:], "w3q0")]
+
+        bt = [keep.tile([P, PACK, J], F32, name="bt%d" % b) for b in range(2)]
+        for b in range(2):
+            for t in range(PACK):
+                c0 = PASS * b + P * t
+                rows = first_stage_rows(
+                    [(w2c[:].bitcast(U8)[:, 2 * c0 : 2 * (c0 + P)].bitcast(FP4X4), w2s[:, c0 : c0 + P],
+                      [v[:].bitcast(FP8X4) for v in v2], halves(s2))], 1)
+                nc.vector.tensor_copy(bt[b][:, t, :], rows[:].indirect(p2[:]))
+
+        w3_rounded.append(round_weight(w3_raw[1]))
+        v3 = gather(t3_win, o3[:], U32, "v3")
+        w3q.append(quantize(w3_rounded[1][:], "w3q1"))
+        step2 = [keep.tile([P, PACK, J], F32, name="step2_%d" % b) for b in range(2)]
+        w1q = {}
+        for b in range(2):
+            codes, scales = w3q[b]
+            for t in range(PACK):
+                cols = slice(P * t, P * (t + 1))
+                rows = first_stage_rows(
+                    [(codes[:, cols].bitcast(FP8X4), scales[:, cols],
+                      [h.bitcast(FP8X4) for h in halves(v3)], halves(s3))], -1)
+                nc.vector.tensor_tensor(step2[b][:, t, :], rows[:].indirect(p3[:]), bt[b][:, t, :], ALU.add)
+            for a in range(2):
+                w1q[a, b] = round_weight(w1_raw[a, b])
+            for a in range(2):
+                w1q[a, b] = quantize(w1q[a, b][:], "w1q%d%d" % (a, b))
+
+        w4c = keep.tile([P, 2, N], U32, name="w4c", align_bytes=64)
+        nc.scalar.copy(
+            out=w4c[:].rearrange("p a (t m) -> p a m t", t=PACK),
+            in_=w4_raw[:].rearrange("p a (m t) -> p a m t", t=PACK),
+        )
+        w4s = keep.tile([P, N], U8, name="w4s", align_bytes=64)
+        nc.vector.tensor_copy(
+            out=w4s[:].rearrange("p (t m) -> p m t", t=PACK),
+            in_=w4s_raw[:].rearrange("p (m t) -> p m t", t=PACK),
+        )
+        v1 = [gather(t1_win[a], o1[:], U32, "v1_%d" % a) for a in range(2)]
+
+        y_banks = [psum.tile([P, PACK, QUARTER], F32, name="y_bank%d" % q) for q in range(J // QUARTER)]
+        y_codes = keep.tile([P, J], U32, name="y_codes", align_bytes=64)
+        y_scales = keep.tile([P, J], U8, name="y_scales", align_bytes=64)
+        out_rows = out_0.rearrange("(p t) j -> p t j", t=PACK)
+        out_words = out_1[0].rearrange("p m t -> p (m t)").bitcast(I32)
+
+        def join(step1, b, j0, j1):
+            z = ring.tile([P, PACK * (j1 - j0)], BF16, name="rounded", tag="rounded", bufs=3, align_bytes=64)
+            nc.vector.tensor_tensor(
+                z[:].rearrange("p (c i t) -> p c t i", i=PACK, t=PACK),
+                step1[:, :, j0:j1].rearrange("p t (c i) -> p c t i", i=PACK),
+                step2[b][:, :, j0:j1].rearrange("p t (c i) -> p c t i", i=PACK),
+                ALU.max,
+            )
+            return z
+
+        def project(zq, b, q, z0):
+            codes, scales = zq
+            for t in range(PACK):
+                cols = slice(P * t, P * (t + 1))
+                nc.tensor.matmul_mx(
+                    out=y_banks[q][:, t, :], lhsT=w4c[:, b, cols].bitcast(FP8X4), lhsT_scale=w4s[4 * b : P, cols],
+                    rhs=codes[:, z0 : z0 + QUARTER].bitcast(FP8X4), rhs_scale=scales[:, z0 : z0 + QUARTER],
+                    start=(b == 0 and t == 0), stop=(b == 1 and t == PACK - 1),
+                )
+
+        def a_rows(b, t):
+            cols = slice(P * t, P * (t + 1))
+            return first_stage_rows(
+                [(w1q[a, b][0][:, cols].bitcast(FP8X4), w1q[a, b][1][:, cols],
+                  [h.bitcast(FP8X4) for h in halves(v1[a])], halves(s1, 4 * a)) for a in range(2)], 1)
+
+        step1 = [ring.tile([P, PACK, J], F32, name="raw", tag="raw", bufs=4) for b in range(2)]
+        for t in range(PACK):
+            nc.vector.tensor_tensor(step1[0][:, t, :], a_rows(0, t)[:].indirect(p1[:]), bt[0][:, t, :], ALU.subtract)
+        z0 = join(step1[0], 0, 0, J)
+        for t in range(PACK - 1):
+            nc.vector.tensor_tensor(step1[1][:, t, :], a_rows(1, t)[:].indirect(p1[:]), bt[1][:, t, :], ALU.subtract)
+            if t == 0:
+                zq0 = quantize(z0[:], "zq0")
+                for q in range(J // QUARTER):
+                    project(zq0, 0, q, QUARTER * q)
+        last_rows = a_rows(1, PACK - 1)
+
+        def finish_z(q):
+            j0, j1 = QUARTER * q, QUARTER * (q + 1)
+            nc.vector.tensor_tensor(
+                step1[1][:, PACK - 1, j0:j1], last_rows[:].indirect(p1[:, j0 // 16 : j1 // 16]),
+                bt[1][:, PACK - 1, j0:j1], ALU.subtract)
+            return join(step1[1], 1, j0, j1)
+
+        def emit_y(q):
+            j0, j1 = QUARTER * q, QUARTER * (q + 1)
+            y_rounded = ring.tile([P, PACK * QUARTER], BF16, name="y_rounded", tag="y_rounded", bufs=2, align_bytes=64)
+            nc.scalar.copy(out=y_rounded[:].rearrange("p (n t) -> p n t", t=PACK), in_=y_banks[q][:].rearrange("p t n -> p n t"))
+            y = ring.tile([P, PACK, QUARTER], F32, name="y", tag="y", bufs=4)
+            nc.scalar.copy(out=y[:], in_=y_banks[q][:])
+            nc.sync.dma_start(out=out_rows[:, :, j0:j1], in_=y[:])
+            nc.vector.quantize_mx(out=y_codes[:, j0:j1].bitcast(FP8X4), scales=y_scales[:, j0:j1], in_=y_rounded[:])
+
+        n_q = J // QUARTER
+        z = finish_z(0)
+        for q in range(n_q):
+            z_next = finish_z(q + 1) if q + 1 < n_q else None
+            project(quantize(z[:], "zq1%d" % q), 1, q, 0)
+            if q > 0:
+                emit_y(q - 1)
+            z = z_next
+        nc.sync.dma_start(out=out_words[:, : J - QUARTER], in_=y_codes[:, : J - QUARTER].bitcast(I32))
+        emit_y(n_q - 1)
+        nc.sync.dma_start(out=out_words[:, J - QUARTER :], in_=y_codes[:, J - QUARTER :].bitcast(I32))
+        for quad in range(4):
+            queue = nc.scalar if quad % 2 else nc.sync
+            queue.dma_start(
+                out=out_2[0, 4 * quad : 4 * quad + 4, :].bitcast(I32),
+                in_=y_scales[32 * quad : 32 * quad + 4, :].bitcast(I32),
+            )

@@ -21,6 +21,7 @@ PACK = 4
 PASS = P * PACK
 BANK = 512
 QUARTER = 128
+PIECES = ((0, 2), (2, 1), (3, 1))
 
 
 def tile_list_milk_coldstep_features_kernel(
@@ -33,6 +34,13 @@ def tile_list_milk_coldstep_features_kernel(
         keep = ctx.enter_context(tc.tile_pool(name="keep", bufs=1))
         ring = ctx.enter_context(tc.tile_pool(name="ring", bufs=1))
         psum = ctx.enter_context(tc.psum_pool(name="psum", bufs=1))
+
+        turns = {}
+
+        def in_turn(pool, shape, dtype, kind, slots):
+            turn = turns.get(kind, 0)
+            turns[kind] = turn + 1
+            return pool.tile(shape, dtype, name=kind, tag="%s%d" % (kind, turn % slots), align_bytes=64)
 
         def load_list(dram, name):
             tile = keep.tile(list(dram.shape), U16, name=name)
@@ -69,13 +77,13 @@ def tile_list_milk_coldstep_features_kernel(
                     )
             return plane
 
-        def load_table_words(words, a):
-            tile = ring.tile([P, T], U32, name="table", tag="table", bufs=3)
+        def load_table_words(words, a, slot):
+            tile = ring.tile([P, T], U32, name="table", tag=slot, align_bytes=64)
             nc.sync.dma_start(out=tile[:].bitcast(I32), in_=words[a].rearrange("p t i -> p (t i)").bitcast(I32))
             return tile
 
         def load_weight(w, a, b):
-            tile = ring.tile([P, PACK, PASS], F32, name="raw", tag="raw", bufs=4)
+            tile = in_turn(ring, [P, PACK, PASS], F32, "raw", 4)
             nc.sync.dma_start(
                 out=tile[:],
                 in_=w[PASS * a : PASS * (a + 1), PASS * b : PASS * (b + 1)].rearrange("(p i) c -> p i c", i=PACK),
@@ -83,7 +91,7 @@ def tile_list_milk_coldstep_features_kernel(
             return tile
 
         def round_weight(raw):
-            rounded = ring.tile([P, PACK * PASS], BF16, name="rounded", tag="rounded", bufs=3, align_bytes=64)
+            rounded = in_turn(ring, [P, PACK * PASS], BF16, "rounded", 3)
             nc.scalar.activation(
                 out=rounded[:].rearrange("p (t m i) -> p m i t", t=PACK, i=PACK),
                 in_=raw[:].rearrange("p i (m t) -> p m i t", t=PACK),
@@ -91,11 +99,12 @@ def tile_list_milk_coldstep_features_kernel(
             )
             return rounded
 
-        def quantize(rounded, name):
+        def quantize(rounded, name, codes=None):
             width = rounded.shape[1] // PACK
-            codes = keep.tile([P, width], U32, name=name + "_codes", align_bytes=64)
+            if codes is None:
+                codes = keep.tile([P, width], U32, name=name + "_codes", align_bytes=64)[:]
             scales = keep.tile([P, width], U8, name=name + "_scales", align_bytes=64)
-            nc.vector.quantize_mx(out=codes[:].bitcast(FP8X4), scales=scales[:], in_=rounded)
+            nc.vector.quantize_mx(out=codes.bitcast(FP8X4), scales=scales[:], in_=rounded)
             return codes, scales
 
         def gather(window, offsets, dtype, name):
@@ -103,10 +112,14 @@ def tile_list_milk_coldstep_features_kernel(
             nc.vector.tensor_copy(picked[:], window[:].indirect(offsets))
             return picked
 
-        def first_stage_rows(passes, sign):
-            rows = ring.tile([P, S], F32, name="rows", tag="rows", bufs=6)
+        def first_stage_rows(passes, sign, slot=None):
+            if slot:
+                turns["rows"] = turns["rows"] + 1
+                rows = ring.tile([P, S], F32, name="rows", tag=slot, align_bytes=64)
+            else:
+                rows = in_turn(ring, [P, S], F32, "rows", 8)
             for half in range(S // BANK):
-                bank = psum.tile([P, BANK], F32, name="bank", tag="bank", bufs=4)
+                bank = psum.tile([P, BANK], F32, name="bank", tag="bank%d" % (turns["rows"] % 2 * 2 + half))
                 for a, (lhsT, lhsT_scale, moving, moving_scale) in enumerate(passes):
                     nc.tensor.matmul_mx(
                         out=bank[:], lhsT=lhsT, lhsT_scale=lhsT_scale, rhs=moving[half], rhs_scale=moving_scale[half],
@@ -129,84 +142,84 @@ def tile_list_milk_coldstep_features_kernel(
         w4s_raw = zeroed_plane(N, "w4s_raw", nc.vector)
 
         o2 = load_list(offs2, "o2")
-        load_scale_rows(nc.sync, s2_win, tab2_scales, 0)
+        load_spread_rows(nc.sync, s2_win, tab2_scales)
         o3 = load_list(offs3, "o3")
+        load_spread_rows(nc.sync, s3_win, tab3_scales)
+        t2_win = load_table_words(tab2_words, 0, "big0")
         w2_raw = keep.tile([P, H], U16, name="w2_raw")
         nc.sync.dma_start(out=w2_raw[:].bitcast(I32), in_=w2_words[0].bitcast(I32))
-        p2 = load_list(pos2, "p2")
-        load_spread_rows(nc.sync, s3_win, tab3_scales)
-        o1 = load_list(offs, "o1")
-        t2_win = load_table_words(tab2_words, 0)
         load_scale_rows(nc.sync, w2s_raw, w2_scales, 0)
+        o1 = load_list(offs, "o1")
         load_spread_rows(nc.sync, s1_win, tab_scales)
-        w3_raw = [load_weight(w3, 0, b) for b in range(2)]
-        t3_win = load_table_words(tab3_words, 0)
+        p2 = load_list(pos2, "p2")
+        w3_raw = [load_weight(w3, 0, 0)]
+        t3_win = load_table_words(tab3_words, 0, "big1")
+        w3_raw.append(load_weight(w3, 0, 1))
         p3 = load_list(pos3, "p3")
+        w1_raw = {(a, 0): load_weight(w1, a, 0) for a in range(2)}
+        t1_win = [load_table_words(tab_words, 0, "big2")]
+        w1_raw[0, 1] = load_weight(w1, 0, 1)
+        t1_win.append(load_table_words(tab_words, 1, "big0"))
+        w1_raw[1, 1] = load_weight(w1, 1, 1)
         p1 = load_list(pos1, "p1")
-        w1_raw = {}
-        for b in range(2):
-            for a in range(2):
-                w1_raw[a, b] = load_weight(w1, a, b)
         load_scale_rows(nc.sync, w4s_raw, w4_scales, 0)
         w4_raw = keep.tile([P, 2, N], U32, name="w4_raw")
         nc.sync.dma_start(out=w4_raw[:].bitcast(I32), in_=w4_words.rearrange("a p c i -> p a (c i)").bitcast(I32))
-        t1_win = [load_table_words(tab_words, a) for a in range(2)]
 
-        s2 = gather(s2_win, o2[:], U8, "s2")
+        s2 = place_rows(nc.scalar, gather(s2_win, o2[:], U8, "s2_picked"), 1, "s2")
         s3 = place_rows(nc.gpsimd, gather(s3_win, o3[:], U8, "s3_picked"), 1, "s3")
-        w3_rounded = [round_weight(w3_raw[0])]
         w2c = keep.tile([P, H], U16, name="w2c", align_bytes=64)
         nc.scalar.copy(
             out=w2c[:].rearrange("p (b t m) -> p b m t", b=2, t=PACK),
             in_=w2_raw[:].rearrange("p (b m t) -> p b m t", b=2, t=PACK),
         )
+        v2 = [gather(t2_win, o2[:, 0:32], U32, "v2_0")]
         w2s = keep.tile([P, H], U8, name="w2s", align_bytes=64)
         nc.vector.tensor_copy(
             out=w2s[:].rearrange("p (b t m) -> p b m t", b=2, t=PACK),
             in_=w2s_raw[:].rearrange("p (b m t) -> p b m t", b=2, t=PACK),
         )
-        v2 = [gather(t2_win, o2[:, 32 * h : 32 * (h + 1)], U32, "v2_%d" % h) for h in range(2)]
+        v2.append(gather(t2_win, o2[:, 32:64], U32, "v2_1"))
         s1 = place_rows(nc.gpsimd, gather(s1_win, o1[:], U8, "s1_picked"), 2, "s1")
-        w3q = [quantize(w3_rounded[0][:], "w3q0")]
+        w3q = []
 
-        bt = [keep.tile([P, PACK, J], F32, name="bt%d" % b) for b in range(2)]
+        bt = []
         for b in range(2):
+            if b == 0:
+                bt.append(keep.tile([P, PACK, J], F32, name="bt0"))
+            else:
+                v3 = gather(t3_win, o3[:], U32, "v3")
+                bt.append(ring.tile([P, PACK, J], F32, name="bt1", tag="big1", align_bytes=64))
             for t in range(PACK):
                 c0 = PASS * b + P * t
                 rows = first_stage_rows(
                     [(w2c[:].bitcast(U8)[:, 2 * c0 : 2 * (c0 + P)].bitcast(FP4X4), w2s[:, c0 : c0 + P],
                       [v[:].bitcast(FP8X4) for v in v2], halves(s2))], 1)
                 nc.vector.tensor_copy(bt[b][:, t, :], rows[:].indirect(p2[:]))
+            w3q.append(quantize(round_weight(w3_raw[b])[:], "w3q%d" % b))
 
-        w3_rounded.append(round_weight(w3_raw[1]))
-        v3 = gather(t3_win, o3[:], U32, "v3")
-        w3q.append(quantize(w3_rounded[1][:], "w3q1"))
-        step2 = [keep.tile([P, PACK, J], F32, name="step2_%d" % b) for b in range(2)]
+        step2 = []
         w1q = {}
+        v1 = []
         for b in range(2):
             codes, scales = w3q[b]
+            if b == 0:
+                step2.append(keep.tile([P, PACK, J], F32, name="step2_0"))
+            else:
+                step2.append(ring.tile([P, PACK, J], F32, name="step2_1", tag="big0", align_bytes=64))
             for t in range(PACK):
                 cols = slice(P * t, P * (t + 1))
                 rows = first_stage_rows(
                     [(codes[:, cols].bitcast(FP8X4), scales[:, cols],
-                      [h.bitcast(FP8X4) for h in halves(v3)], halves(s3))], -1)
+                      [h.bitcast(FP8X4) for h in halves(v3)], halves(s3))], -1, "last_d" if (b, t) == (1, PACK - 1) else None)
                 nc.vector.tensor_tensor(step2[b][:, t, :], rows[:].indirect(p3[:]), bt[b][:, t, :], ALU.add)
+            if b == 0:
+                v1.append(gather(t1_win[0], o1[:], U32, "v1_0"))
+            w1_codes = ring.tile([P, 2, PASS], U32, name="w1_codes", tag=("big2", "last_d")[b], align_bytes=64)
             for a in range(2):
-                w1q[a, b] = round_weight(w1_raw[a, b])
-            for a in range(2):
-                w1q[a, b] = quantize(w1q[a, b][:], "w1q%d%d" % (a, b))
-
-        w4c = keep.tile([P, 2, N], U32, name="w4c", align_bytes=64)
-        nc.scalar.copy(
-            out=w4c[:].rearrange("p a (t m) -> p a m t", t=PACK),
-            in_=w4_raw[:].rearrange("p a (m t) -> p a m t", t=PACK),
-        )
-        w4s = keep.tile([P, N], U8, name="w4s", align_bytes=64)
-        nc.vector.tensor_copy(
-            out=w4s[:].rearrange("p (t m) -> p m t", t=PACK),
-            in_=w4s_raw[:].rearrange("p (m t) -> p m t", t=PACK),
-        )
-        v1 = [gather(t1_win[a], o1[:], U32, "v1_%d" % a) for a in range(2)]
+                w1q[a, b] = quantize(round_weight(w1_raw[a, b])[:], "w1q%d%d" % (a, b), w1_codes[:, a, :])
+            if b == 0:
+                v1.append(gather(t1_win[1], o1[:], U32, "v1_1"))
 
         y_banks = [psum.tile([P, PACK, QUARTER], F32, name="y_bank%d" % q) for q in range(J // QUARTER)]
         y_codes = keep.tile([P, J], U32, name="y_codes", align_bytes=64)
@@ -215,7 +228,7 @@ def tile_list_milk_coldstep_features_kernel(
         out_words = out_1[0].rearrange("p m t -> p (m t)").bitcast(I32)
 
         def join(step1, b, j0, j1):
-            z = ring.tile([P, PACK * (j1 - j0)], BF16, name="rounded", tag="rounded", bufs=3, align_bytes=64)
+            z = in_turn(ring, [P, PACK * (j1 - j0)], BF16, "rounded", 3)
             nc.vector.tensor_tensor(
                 z[:].rearrange("p (c i t) -> p c t i", i=PACK, t=PACK),
                 step1[:, :, j0:j1].rearrange("p t (c i) -> p c t i", i=PACK),
@@ -240,45 +253,59 @@ def tile_list_milk_coldstep_features_kernel(
                 [(w1q[a, b][0][:, cols].bitcast(FP8X4), w1q[a, b][1][:, cols],
                   [h.bitcast(FP8X4) for h in halves(v1[a])], halves(s1, 4 * a)) for a in range(2)], 1)
 
-        step1 = [ring.tile([P, PACK, J], F32, name="raw", tag="raw", bufs=4) for b in range(2)]
+        step1 = [in_turn(ring, [P, PACK, J], F32, "raw", 4) for b in range(2)]
         for t in range(PACK):
             nc.vector.tensor_tensor(step1[0][:, t, :], a_rows(0, t)[:].indirect(p1[:]), bt[0][:, t, :], ALU.subtract)
+        w4c = keep.tile([P, 2, N], U32, name="w4c", align_bytes=64)
+        nc.scalar.copy(
+            out=w4c[:].rearrange("p a (t m) -> p a m t", t=PACK),
+            in_=w4_raw[:].rearrange("p a (m t) -> p a m t", t=PACK),
+        )
+        w4s = keep.tile([P, N], U8, name="w4s", align_bytes=64)
+        nc.vector.tensor_copy(
+            out=w4s[:].rearrange("p (t m) -> p m t", t=PACK),
+            in_=w4s_raw[:].rearrange("p (m t) -> p m t", t=PACK),
+        )
         z0 = join(step1[0], 0, 0, J)
-        for t in range(PACK - 1):
-            nc.vector.tensor_tensor(step1[1][:, t, :], a_rows(1, t)[:].indirect(p1[:]), bt[1][:, t, :], ALU.subtract)
-            if t == 0:
-                zq0 = quantize(z0[:], "zq0")
-                for q in range(J // QUARTER):
-                    project(zq0, 0, q, QUARTER * q)
-        last_rows = a_rows(1, PACK - 1)
+        last_rows = [a_rows(1, t) for t in range(PACK)]
 
-        def finish_z(q):
-            j0, j1 = QUARTER * q, QUARTER * (q + 1)
-            nc.vector.tensor_tensor(
-                step1[1][:, PACK - 1, j0:j1], last_rows[:].indirect(p1[:, j0 // 16 : j1 // 16]),
-                bt[1][:, PACK - 1, j0:j1], ALU.subtract)
+        def finish_z(j0, j1):
+            for t in range(PACK):
+                nc.vector.tensor_tensor(
+                    step1[1][:, t, j0:j1], last_rows[t][:].indirect(p1[:, j0 // 16 : j1 // 16]),
+                    bt[1][:, t, j0:j1], ALU.subtract)
             return join(step1[1], 1, j0, j1)
 
-        def emit_y(q):
-            j0, j1 = QUARTER * q, QUARTER * (q + 1)
-            y_rounded = ring.tile([P, PACK * QUARTER], BF16, name="y_rounded", tag="y_rounded", bufs=2, align_bytes=64)
-            nc.scalar.copy(out=y_rounded[:].rearrange("p (n t) -> p n t", t=PACK), in_=y_banks[q][:].rearrange("p t n -> p n t"))
-            y = ring.tile([P, PACK, QUARTER], F32, name="y", tag="y", bufs=4)
+        def store_y(q):
+            y = in_turn(ring, [P, PACK, QUARTER], F32, "y", 4)
             nc.scalar.copy(out=y[:], in_=y_banks[q][:])
-            nc.sync.dma_start(out=out_rows[:, :, j0:j1], in_=y[:])
-            nc.vector.quantize_mx(out=y_codes[:, j0:j1].bitcast(FP8X4), scales=y_scales[:, j0:j1], in_=y_rounded[:])
+            nc.sync.dma_start(out=out_rows[:, :, QUARTER * q : QUARTER * (q + 1)], in_=y[:])
 
-        n_q = J // QUARTER
-        z = finish_z(0)
-        for q in range(n_q):
-            z_next = finish_z(q + 1) if q + 1 < n_q else None
-            project(quantize(z[:], "zq1%d" % q), 1, q, 0)
-            if q > 0:
-                emit_y(q - 1)
-            z = z_next
-        nc.sync.dma_start(out=out_words[:, : J - QUARTER], in_=y_codes[:, : J - QUARTER].bitcast(I32))
-        emit_y(n_q - 1)
-        nc.sync.dma_start(out=out_words[:, J - QUARTER :], in_=y_codes[:, J - QUARTER :].bitcast(I32))
+        def store_codes(y_rounded, j0, j1):
+            nc.vector.quantize_mx(out=y_codes[:, j0:j1].bitcast(FP8X4), scales=y_scales[:, j0:j1], in_=y_rounded[:])
+            nc.sync.dma_start(out=out_words[:, j0:j1], in_=y_codes[:, j0:j1].bitcast(I32))
+
+        zq0 = quantize(z0[:], "zq0")
+        for q in range(J // QUARTER):
+            project(zq0, 0, q, QUARTER * q)
+        last_q = J // QUARTER - 1
+        y_early = keep.tile([P, PACK * QUARTER * last_q], BF16, name="y_early", align_bytes=64)
+        y_last = keep.tile([P, PACK * QUARTER], BF16, name="y_last", align_bytes=64)
+        for first, count in PIECES:
+            z = finish_z(QUARTER * first, QUARTER * (first + count))
+            zq = quantize(z[:], "zq1%d" % first)
+            for q in range(first, first + count):
+                project(zq, 1, q, QUARTER * (q - first))
+            for q in range(first, first + count):
+                by_column = y_banks[q][:].rearrange("p t n -> p n t")
+                if q < last_q:
+                    cols = y_early[:, PACK * QUARTER * q : PACK * QUARTER * (q + 1)]
+                    nc.scalar.copy(out=cols.rearrange("p (n t) -> p n t", t=PACK), in_=by_column)
+                    store_y(q)
+        store_codes(y_early, 0, QUARTER * last_q)
+        nc.vector.tensor_copy(out=y_last[:].rearrange("p (n t) -> p n t", t=PACK), in_=by_column)
+        store_y(last_q)
+        store_codes(y_last, QUARTER * last_q, J)
         for quad in range(4):
             queue = nc.scalar if quad % 2 else nc.sync
             queue.dma_start(

@@ -145,15 +145,16 @@ def tile_list_milk_coldstep_features_kernel(
         load_spread_rows(nc.sync, s2_win, tab2_scales)
         o3 = load_list(offs3, "o3")
         load_spread_rows(nc.sync, s3_win, tab3_scales)
-        t2_win = load_table_words(tab2_words, 0, "big0")
         w2_raw = keep.tile([P, H], U16, name="w2_raw")
         nc.sync.dma_start(out=w2_raw[:].bitcast(I32), in_=w2_words[0].bitcast(I32))
         load_scale_rows(nc.sync, w2s_raw, w2_scales, 0)
+        w3_raw = [load_weight(w3, 0, 0)]
+        t2_win = load_table_words(tab2_words, 0, "big0")
+        s2 = place_rows(nc.sync, gather(s2_win, o2[:], U8, "s2_picked"), 1, "s2")
         o1 = load_list(offs, "o1")
         load_spread_rows(nc.sync, s1_win, tab_scales)
-        p2 = load_list(pos2, "p2")
-        w3_raw = [load_weight(w3, 0, 0)]
         t3_win = load_table_words(tab3_words, 0, "big1")
+        p2 = load_list(pos2, "p2")
         w3_raw.append(load_weight(w3, 0, 1))
         p3 = load_list(pos3, "p3")
         w1_raw = {(a, 0): load_weight(w1, a, 0) for a in range(2)}
@@ -166,7 +167,6 @@ def tile_list_milk_coldstep_features_kernel(
         w4_raw = keep.tile([P, 2, N], U32, name="w4_raw")
         nc.sync.dma_start(out=w4_raw[:].bitcast(I32), in_=w4_words.rearrange("a p c i -> p a (c i)").bitcast(I32))
 
-        s2 = place_rows(nc.scalar, gather(s2_win, o2[:], U8, "s2_picked"), 1, "s2")
         s3 = place_rows(nc.gpsimd, gather(s3_win, o3[:], U8, "s3_picked"), 1, "s3")
         w2c = keep.tile([P, H], U16, name="w2c", align_bytes=64)
         nc.scalar.copy(
@@ -280,6 +280,7 @@ def tile_list_milk_coldstep_features_kernel(
             y = in_turn(ring, [P, PACK, QUARTER], F32, "y", 4)
             nc.scalar.copy(out=y[:], in_=y_banks[q][:])
             nc.sync.dma_start(out=out_rows[:, :, QUARTER * q : QUARTER * (q + 1)], in_=y[:])
+            return y
 
         def store_codes(y_rounded, j0, j1):
             nc.vector.quantize_mx(out=y_codes[:, j0:j1].bitcast(FP8X4), scales=y_scales[:, j0:j1], in_=y_rounded[:])
@@ -303,8 +304,10 @@ def tile_list_milk_coldstep_features_kernel(
                     nc.scalar.copy(out=cols.rearrange("p (n t) -> p n t", t=PACK), in_=by_column)
                     store_y(q)
         store_codes(y_early, 0, QUARTER * last_q)
-        nc.vector.tensor_copy(out=y_last[:].rearrange("p (n t) -> p n t", t=PACK), in_=by_column)
-        store_y(last_q)
+        nc.vector.tensor_copy(
+            out=y_last[:].rearrange("p (c i t) -> p c t i", i=PACK, t=PACK),
+            in_=store_y(last_q)[:].rearrange("p t (c i) -> p c t i", i=PACK),
+        )
         store_codes(y_last, QUARTER * last_q, J)
         for quad in range(4):
             queue = nc.scalar if quad % 2 else nc.sync

@@ -222,16 +222,18 @@ def tile_list_milk_coldstep_features_kernel(
                 v1.append(gather(t1_win[1], o1[:], U32, "v1_1"))
 
         y_banks = [psum.tile([P, PACK, QUARTER], F32, name="y_bank%d" % q) for q in range(J // QUARTER)]
-        y_codes = keep.tile([P, J], U32, name="y_codes", align_bytes=64)
         y_scales = keep.tile([P, J], U8, name="y_scales", align_bytes=64)
         out_rows = out_0.rearrange("(p t) j -> p t j", t=PACK)
         out_words = out_1[0].rearrange("p m t -> p (m t)").bitcast(I32)
 
         def join(step1, b, j0, j1):
-            z = in_turn(ring, [P, PACK * (j1 - j0)], BF16, "rounded", 3)
+            if (b, j1 - j0, j1) == (1, QUARTER, J):
+                z = ring.tile([P, PACK * QUARTER], BF16, name="z_last", tag="last_z", align_bytes=64)
+            else:
+                z = in_turn(ring, [P, PACK * (j1 - j0)], BF16, "rounded", 3)
             nc.vector.tensor_tensor(
                 z[:].rearrange("p (c i t) -> p c t i", i=PACK, t=PACK),
-                step1[:, :, j0:j1].rearrange("p t (c i) -> p c t i", i=PACK),
+                step1[:].rearrange("p t (c i) -> p c t i", i=PACK),
                 step2[b][:, :, j0:j1].rearrange("p t (c i) -> p c t i", i=PACK),
                 ALU.max,
             )
@@ -253,9 +255,9 @@ def tile_list_milk_coldstep_features_kernel(
                 [(w1q[a, b][0][:, cols].bitcast(FP8X4), w1q[a, b][1][:, cols],
                   [h.bitcast(FP8X4) for h in halves(v1[a])], halves(s1, 4 * a)) for a in range(2)], 1)
 
-        step1 = [in_turn(ring, [P, PACK, J], F32, "raw", 4) for b in range(2)]
+        step1 = in_turn(ring, [P, PACK, J], F32, "raw", 4)
         for t in range(PACK):
-            nc.vector.tensor_tensor(step1[0][:, t, :], a_rows(0, t)[:].indirect(p1[:]), bt[0][:, t, :], ALU.subtract)
+            nc.vector.tensor_tensor(step1[:, t, :], a_rows(0, t)[:].indirect(p1[:]), bt[0][:, t, :], ALU.subtract)
         w4c = keep.tile([P, 2, N], U32, name="w4c", align_bytes=64)
         nc.scalar.copy(
             out=w4c[:].rearrange("p a (t m) -> p a m t", t=PACK),
@@ -266,15 +268,16 @@ def tile_list_milk_coldstep_features_kernel(
             out=w4s[:].rearrange("p (t m) -> p m t", t=PACK),
             in_=w4s_raw[:].rearrange("p (m t) -> p m t", t=PACK),
         )
-        z0 = join(step1[0], 0, 0, J)
+        z0 = join(step1, 0, 0, J)
         last_rows = [a_rows(1, t) for t in range(PACK)]
 
         def finish_z(j0, j1):
+            piece = ring.tile([P, PACK, j1 - j0], F32, name="piece", tag="piece", align_bytes=64)
             for t in range(PACK):
                 nc.vector.tensor_tensor(
-                    step1[1][:, t, j0:j1], last_rows[t][:].indirect(p1[:, j0 // 16 : j1 // 16]),
+                    piece[:, t, :], last_rows[t][:].indirect(p1[:, j0 // 16 : j1 // 16]),
                     bt[1][:, t, j0:j1], ALU.subtract)
-            return join(step1[1], 1, j0, j1)
+            return join(piece, 1, j0, j1)
 
         def store_y(q):
             y = in_turn(ring, [P, PACK, QUARTER], F32, "y", 4)
@@ -303,6 +306,7 @@ def tile_list_milk_coldstep_features_kernel(
                     cols = y_early[:, PACK * QUARTER * q : PACK * QUARTER * (q + 1)]
                     nc.scalar.copy(out=cols.rearrange("p (n t) -> p n t", t=PACK), in_=by_column)
                     store_y(q)
+        y_codes = ring.tile([P, J], U32, name="y_codes", tag="last_z", align_bytes=64)
         store_codes(y_early, 0, QUARTER * last_q)
         nc.vector.tensor_copy(
             out=y_last[:].rearrange("p (c i t) -> p c t i", i=PACK, t=PACK),

@@ -19,9 +19,18 @@ COPY = mybir.ActivationFunctionType.Copy
 P = 128
 PACK = 4
 PASS = P * PACK
+A_PASSES = K // PASS
+GROUPS = H // PASS
 BANK = 512
-QUARTER = 128
+QUADS, QUAD = 4, 32
+BLOCKS = PASS // 32
+QUAD_BLOCKS = BLOCKS // QUADS
+LIST_ROWS = 16
+LINE = 4
+QUARTER = BANK // PACK
+QUARTERS = J // QUARTER
 PIECES = ((0, 2), (2, 1), (3, 1))
+RAW_SLOTS, ROUNDED_SLOTS, ROW_SLOTS = 4, 4, GROUPS * PACK
 
 
 def tile_list_milk_coldstep_features_kernel(
@@ -37,61 +46,65 @@ def tile_list_milk_coldstep_features_kernel(
 
         turns = {}
 
-        def in_turn(pool, shape, dtype, kind, slots):
-            turn = turns.get(kind, 0)
-            turns[kind] = turn + 1
-            return pool.tile(shape, dtype, name=kind, tag="%s%d" % (kind, turn % slots), align_bytes=64)
+        def next_turn(kind):
+            turns[kind] = turns.get(kind, 0) + 1
+            return turns[kind] - 1
+
+        def shared(shape, dtype, name, slot):
+            return ring.tile(shape, dtype, name=name, tag=slot, align_bytes=64)
+
+        def in_turn(shape, dtype, kind, slots):
+            return shared(shape, dtype, kind, "%s%d" % (kind, next_turn(kind) % slots))
 
         def load_list(dram, name):
             tile = keep.tile(list(dram.shape), U16, name=name)
             nc.sync.dma_start(tile[:], dram)
             return tile
 
-        def zeroed_plane(width, name, engine):
+        def zeroed_bytes(width, name):
             tile = keep.tile([P, width], U8, name=name, align_bytes=64)
-            engine.memset(tile[:].bitcast(I32), 0)
+            nc.vector.memset(tile[:].bitcast(I32), 0)
             return tile
 
-        def load_scale_rows(queue, plane, scales, first):
+        def load_plane(plane, scales):
             passes = scales.shape[0]
-            for quad in range(4):
-                rows = scales[:, 4 * quad : 4 * quad + 4, :] if passes > 1 else scales[0, 4 * quad : 4 * quad + 4, :]
-                queue.dma_start(
-                    out=plane[32 * quad + first : 32 * quad + first + 4 * passes, :].bitcast(I32),
-                    in_=rows.bitcast(I32),
+            for quad in range(QUADS):
+                blocks = slice(QUAD_BLOCKS * quad, QUAD_BLOCKS * (quad + 1))
+                source = scales[:, blocks, :] if passes > 1 else scales[0, blocks, :]
+                nc.sync.dma_start(
+                    out=plane[QUAD * quad : QUAD * quad + QUAD_BLOCKS * passes, :].bitcast(I32),
+                    in_=source.bitcast(I32),
                 )
 
-        def load_spread_rows(queue, window, scales):
-            rows = scales.rearrange("a q t -> (a q) t")
-            queue.dma_start(out=window[0 : P : P // rows.shape[0], :].bitcast(I32), in_=rows.bitcast(I32))
+        def load_spread(window, scales):
+            source = scales.rearrange("g b c -> (g b) c")
+            nc.sync.dma_start(out=window[0 : P : P // source.shape[0], :].bitcast(I32), in_=source.bitcast(I32))
 
-        def place_rows(queue, picked, passes, name):
-            plane = zeroed_plane(S, name, nc.vector)
-            step = P // (16 * passes)
-            for a in range(passes):
-                for r in range(4):
-                    first = step * (16 * a + r)
-                    queue.dma_start(
-                        out=plane[4 * a + r : P : 32, :].bitcast(I32),
-                        in_=picked[first : first + 12 * step + 1 : 4 * step, :].bitcast(I32),
-                    )
-            return plane
+        def place_rows(plane, picked, passes, kp):
+            spacing = P // (BLOCKS * passes)
+            for e in range(QUAD_BLOCKS):
+                low = spacing * (BLOCKS * kp + e)
+                high = low + (QUADS - 1) * QUAD_BLOCKS * spacing
+                nc.sync.dma_start(
+                    out=plane[QUAD_BLOCKS * kp + e : P : QUAD, :].bitcast(I32),
+                    in_=picked[low : high + 1 : QUAD_BLOCKS * spacing, :].bitcast(I32),
+                )
 
-        def load_table_words(words, a, slot):
-            tile = ring.tile([P, T], U32, name="table", tag=slot, align_bytes=64)
-            nc.sync.dma_start(out=tile[:].bitcast(I32), in_=words[a].rearrange("p t i -> p (t i)").bitcast(I32))
+        def load_table_words(words, kp, slot):
+            tile = shared([P, T], U32, "table", slot)
+            nc.sync.dma_start(out=tile[:].bitcast(I32), in_=words[kp].rearrange("p c i -> p (c i)").bitcast(I32))
             return tile
 
-        def load_weight(w, a, b):
-            tile = in_turn(ring, [P, PACK, PASS], F32, "raw", 4)
+        def load_weight(w, kp, g):
+            tile = in_turn([P, PACK, PASS], F32, "raw", RAW_SLOTS)
             nc.sync.dma_start(
                 out=tile[:],
-                in_=w[PASS * a : PASS * (a + 1), PASS * b : PASS * (b + 1)].rearrange("(p i) c -> p i c", i=PACK),
+                in_=w[PASS * kp : PASS * (kp + 1), PASS * g : PASS * (g + 1)].rearrange("(p i) c -> p i c", i=PACK),
             )
             return tile
 
         def round_weight(raw):
-            rounded = in_turn(ring, [P, PACK * PASS], BF16, "rounded", 3)
+            rounded = in_turn([P, PACK * PASS], BF16, "rounded", ROUNDED_SLOTS)
             nc.scalar.activation(
                 out=rounded[:].rearrange("p (t m i) -> p m i t", t=PACK, i=PACK),
                 in_=raw[:].rearrange("p i (m t) -> p m i t", t=PACK),
@@ -108,179 +121,185 @@ def tile_list_milk_coldstep_features_kernel(
             return codes, scales
 
         def gather(window, offsets, dtype, name):
-            picked = keep.tile([P, 16 * offsets.shape[1]], dtype, name=name, align_bytes=64)
+            picked = keep.tile([P, LIST_ROWS * offsets.shape[1]], dtype, name=name, align_bytes=64)
             nc.vector.tensor_copy(picked[:], window[:].indirect(offsets))
             return picked
-
-        def first_stage_rows(passes, sign, slot=None):
-            if slot:
-                turns["rows"] = turns["rows"] + 1
-                rows = ring.tile([P, S], F32, name="rows", tag=slot, align_bytes=64)
-            else:
-                rows = in_turn(ring, [P, S], F32, "rows", 8)
-            for half in range(S // BANK):
-                bank = psum.tile([P, BANK], F32, name="bank", tag="bank%d" % (turns["rows"] % 2 * 2 + half))
-                for a, (lhsT, lhsT_scale, moving, moving_scale) in enumerate(passes):
-                    nc.tensor.matmul_mx(
-                        out=bank[:], lhsT=lhsT, lhsT_scale=lhsT_scale, rhs=moving[half], rhs_scale=moving_scale[half],
-                        start=(a == 0), stop=(a == len(passes) - 1),
-                    )
-                cols = rows[:, BANK * half : BANK * (half + 1)]
-                if sign > 0:
-                    nc.scalar.copy(out=cols, in_=bank[:])
-                else:
-                    nc.scalar.activation(out=cols, in_=bank[:], func=COPY, scale=-1.0)
-            return rows
 
         def halves(tile, first_row=0):
             return [tile[first_row:P, BANK * h : BANK * (h + 1)] for h in range(S // BANK)]
 
-        s2_win = zeroed_plane(T, "s2_win", nc.vector)
-        s3_win = zeroed_plane(T, "s3_win", nc.vector)
-        w2s_raw = zeroed_plane(H, "w2s_raw", nc.vector)
-        s1_win = zeroed_plane(T, "s1_win", nc.vector)
-        w4s_raw = zeroed_plane(N, "w4s_raw", nc.vector)
+        def slice_rows(operands, negate=False, slot=None):
+            turn = next_turn("rows")
+            rows = shared([P, S], F32, "rows", slot or "rows%d" % (turn % ROW_SLOTS))
+            for half in range(S // BANK):
+                bank = psum.tile([P, BANK], F32, name="bank", tag="bank%d" % ((turn + 1) % 2 * 2 + half))
+                for kp, (lhsT, lhsT_scale, moving, moving_scale) in enumerate(operands):
+                    nc.tensor.matmul_mx(
+                        out=bank[:], lhsT=lhsT, lhsT_scale=lhsT_scale, rhs=moving[half], rhs_scale=moving_scale[half],
+                        start=(kp == 0), stop=(kp == len(operands) - 1),
+                    )
+                cols = rows[:, BANK * half : BANK * (half + 1)]
+                if negate:
+                    nc.scalar.activation(out=cols, in_=bank[:], func=COPY, scale=-1.0)
+                else:
+                    nc.scalar.copy(out=cols, in_=bank[:])
+            return rows
+
+        s2_win = zeroed_bytes(T, "s2_win")
+        s3_win = zeroed_bytes(T, "s3_win")
+        w2s_raw = zeroed_bytes(H, "w2s_raw")
+        s1_win = zeroed_bytes(T, "s1_win")
+        w4s_raw = zeroed_bytes(N, "w4s_raw")
+        s2, s3, s1 = [zeroed_bytes(S, name) for name in ("s2", "s3", "s1")]
 
         o2 = load_list(offs2, "o2")
-        load_spread_rows(nc.sync, s2_win, tab2_scales)
+        load_spread(s2_win, tab2_scales)
         o3 = load_list(offs3, "o3")
-        load_spread_rows(nc.sync, s3_win, tab3_scales)
+        load_spread(s3_win, tab3_scales)
         w2_raw = keep.tile([P, H], U16, name="w2_raw")
         nc.sync.dma_start(out=w2_raw[:].bitcast(I32), in_=w2_words[0].bitcast(I32))
-        load_scale_rows(nc.sync, w2s_raw, w2_scales, 0)
+        load_plane(w2s_raw, w2_scales)
         w3_raw = [load_weight(w3, 0, 0)]
         t2_win = load_table_words(tab2_words, 0, "big0")
-        s2 = place_rows(nc.sync, gather(s2_win, o2[:], U8, "s2_picked"), 1, "s2")
+        place_rows(s2, gather(s2_win, o2[:], U8, "s2_picked"), 1, 0)
         o1 = load_list(offs, "o1")
-        load_spread_rows(nc.sync, s1_win, tab_scales)
+        load_spread(s1_win, tab_scales)
         t3_win = load_table_words(tab3_words, 0, "big1")
         p2 = load_list(pos2, "p2")
         w3_raw.append(load_weight(w3, 0, 1))
+        place_rows(s3, gather(s3_win, o3[:], U8, "s3_picked"), 1, 0)
         p3 = load_list(pos3, "p3")
-        w1_raw = {(a, 0): load_weight(w1, a, 0) for a in range(2)}
-        t1_win = [load_table_words(tab_words, 0, "big2")]
+        w1_raw = {(0, 0): load_weight(w1, 0, 0)}
+        s1_picked = gather(s1_win, o1[:], U8, "s1_picked")
+        place_rows(s1, s1_picked, A_PASSES, 0)
+        w1_raw[1, 0] = load_weight(w1, 1, 0)
+        place_rows(s1, s1_picked, A_PASSES, 1)
         w1_raw[0, 1] = load_weight(w1, 0, 1)
-        t1_win.append(load_table_words(tab_words, 1, "big0"))
+        t1_win = [load_table_words(tab_words, 0, "big2"), load_table_words(tab_words, 1, "big0")]
         w1_raw[1, 1] = load_weight(w1, 1, 1)
         p1 = load_list(pos1, "p1")
-        load_scale_rows(nc.sync, w4s_raw, w4_scales, 0)
-        w4_raw = keep.tile([P, 2, N], U32, name="w4_raw")
-        nc.sync.dma_start(out=w4_raw[:].bitcast(I32), in_=w4_words.rearrange("a p c i -> p a (c i)").bitcast(I32))
+        load_plane(w4s_raw, w4_scales)
+        w4_raw = keep.tile([P, GROUPS, N], U32, name="w4_raw")
+        nc.sync.dma_start(out=w4_raw[:].bitcast(I32), in_=w4_words.rearrange("g p c i -> p g (c i)").bitcast(I32))
 
-        s3 = place_rows(nc.gpsimd, gather(s3_win, o3[:], U8, "s3_picked"), 1, "s3")
         w2c = keep.tile([P, H], U16, name="w2c", align_bytes=64)
         nc.scalar.copy(
-            out=w2c[:].rearrange("p (b t m) -> p b m t", b=2, t=PACK),
-            in_=w2_raw[:].rearrange("p (b m t) -> p b m t", b=2, t=PACK),
+            out=w2c[:].rearrange("p (g t m) -> p g m t", g=GROUPS, t=PACK),
+            in_=w2_raw[:].rearrange("p (g m t) -> p g m t", g=GROUPS, t=PACK),
         )
-        v2 = [gather(t2_win, o2[:, 0:32], U32, "v2_0")]
+        half_list = BANK // LIST_ROWS
+        v2 = [gather(t2_win, o2[:, :half_list], U32, "v2_0")]
         w2s = keep.tile([P, H], U8, name="w2s", align_bytes=64)
         nc.vector.tensor_copy(
-            out=w2s[:].rearrange("p (b t m) -> p b m t", b=2, t=PACK),
-            in_=w2s_raw[:].rearrange("p (b m t) -> p b m t", b=2, t=PACK),
+            out=w2s[:].rearrange("p (g t m) -> p g m t", g=GROUPS, t=PACK),
+            in_=w2s_raw[:].rearrange("p (g m t) -> p g m t", g=GROUPS, t=PACK),
         )
-        v2.append(gather(t2_win, o2[:, 32:64], U32, "v2_1"))
-        s1 = place_rows(nc.gpsimd, gather(s1_win, o1[:], U8, "s1_picked"), 2, "s1")
-        w3q = []
+        v2.append(gather(t2_win, o2[:, half_list:], U32, "v2_1"))
 
-        bt = []
-        for b in range(2):
-            if b == 0:
-                bt.append(keep.tile([P, PACK, J], F32, name="bt0"))
-            else:
-                v3 = gather(t3_win, o3[:], U32, "v3")
-                bt.append(ring.tile([P, PACK, J], F32, name="bt1", tag="big1", align_bytes=64))
+        def pick_b(g, picked):
             for t in range(PACK):
-                c0 = PASS * b + P * t
-                rows = first_stage_rows(
-                    [(w2c[:].bitcast(U8)[:, 2 * c0 : 2 * (c0 + P)].bitcast(FP4X4), w2s[:, c0 : c0 + P],
-                      [v[:].bitcast(FP8X4) for v in v2], halves(s2))], 1)
-                nc.vector.tensor_copy(bt[b][:, t, :], rows[:].indirect(p2[:]))
-            w3q.append(quantize(round_weight(w3_raw[b])[:], "w3q%d" % b))
+                c0 = PASS * g + P * t
+                rows = slice_rows([(
+                    w2c[:].bitcast(U8)[:, 2 * c0 : 2 * (c0 + P)].bitcast(FP4X4), w2s[:, c0 : c0 + P],
+                    [v[:].bitcast(FP8X4) for v in v2], halves(s2))])
+                nc.vector.tensor_copy(picked[:, t, :], rows[:].indirect(p2[:]))
+            return picked
 
-        step2 = []
-        w1q = {}
-        v1 = []
-        for b in range(2):
-            codes, scales = w3q[b]
-            if b == 0:
-                step2.append(keep.tile([P, PACK, J], F32, name="step2_0"))
-            else:
-                step2.append(ring.tile([P, PACK, J], F32, name="step2_1", tag="big0", align_bytes=64))
+        bt = [pick_b(0, keep.tile([P, PACK, J], F32, name="bt0"))]
+        w3q = [quantize(round_weight(w3_raw[0])[:], "w3q0")]
+        v3 = gather(t3_win, o3[:], U32, "v3")
+        bt.append(pick_b(1, shared([P, PACK, J], F32, "bt1", "big1")))
+
+        def second_step(g, diff, last_slot=None):
+            codes, scales = w3q[g]
             for t in range(PACK):
                 cols = slice(P * t, P * (t + 1))
-                rows = first_stage_rows(
+                rows = slice_rows(
                     [(codes[:, cols].bitcast(FP8X4), scales[:, cols],
-                      [h.bitcast(FP8X4) for h in halves(v3)], halves(s3))], -1, "last_d" if (b, t) == (1, PACK - 1) else None)
-                nc.vector.tensor_tensor(step2[b][:, t, :], rows[:].indirect(p3[:]), bt[b][:, t, :], ALU.add)
-            if b == 0:
-                v1.append(gather(t1_win[0], o1[:], U32, "v1_0"))
-            w1_codes = ring.tile([P, 2, PASS], U32, name="w1_codes", tag=("big2", "last_d")[b], align_bytes=64)
-            for a in range(2):
-                w1q[a, b] = quantize(round_weight(w1_raw[a, b])[:], "w1q%d%d" % (a, b), w1_codes[:, a, :])
-            if b == 0:
-                v1.append(gather(t1_win[1], o1[:], U32, "v1_1"))
+                      [h.bitcast(FP8X4) for h in halves(v3)], halves(s3))],
+                    negate=True, slot=last_slot if t == PACK - 1 else None)
+                nc.vector.tensor_tensor(diff[:, t, :], rows[:].indirect(p3[:]), bt[g][:, t, :], ALU.add)
+            return diff
 
-        y_banks = [psum.tile([P, PACK, QUARTER], F32, name="y_bank%d" % q) for q in range(J // QUARTER)]
+        step2 = [second_step(0, keep.tile([P, PACK, J], F32, name="step2_0"))]
+        v1 = [gather(t1_win[0], o1[:], U32, "v1_0")]
+        codes_mid = shared([P, A_PASSES + 1, PASS], U32, "codes_mid", "big2")
+        w3q.append(quantize(round_weight(w3_raw[1])[:], "w3q1", codes_mid[:, A_PASSES, :]))
+        w1q = {
+            (kp, 0): quantize(round_weight(w1_raw[kp, 0])[:], "w1q%d0" % kp, codes_mid[:, kp, :])
+            for kp in range(A_PASSES)
+        }
+        v1.append(gather(t1_win[1], o1[:], U32, "v1_1"))
+        step2.append(second_step(1, shared([P, PACK, J], F32, "step2_1", "big0"), "last_d"))
+        codes_late = shared([P, A_PASSES, PASS], U32, "codes_late", "last_d")
+        for kp in range(A_PASSES):
+            w1q[kp, 1] = quantize(round_weight(w1_raw[kp, 1])[:], "w1q%d1" % kp, codes_late[:, kp, :])
+
+        y_banks = [psum.tile([P, PACK, QUARTER], F32, name="y_bank%d" % q) for q in range(QUARTERS)]
         y_scales = keep.tile([P, J], U8, name="y_scales", align_bytes=64)
         out_rows = out_0.rearrange("(p t) j -> p t j", t=PACK)
         out_words = out_1[0].rearrange("p m t -> p (m t)").bitcast(I32)
 
-        def join(step1, b, j0, j1):
-            if (b, j1 - j0, j1) == (1, QUARTER, J):
-                z = ring.tile([P, PACK * QUARTER], BF16, name="z_last", tag="last_z", align_bytes=64)
-            else:
-                z = in_turn(ring, [P, PACK * (j1 - j0)], BF16, "rounded", 3)
+        def a_rows(g, t):
+            cols = slice(P * t, P * (t + 1))
+            return slice_rows(
+                [(w1q[kp, g][0][:, cols].bitcast(FP8X4), w1q[kp, g][1][:, cols],
+                  [h.bitcast(FP8X4) for h in halves(v1[kp])], halves(s1, QUAD_BLOCKS * kp))
+                 for kp in range(A_PASSES)])
+
+        def join(z, diff, g, j0, j1):
             nc.vector.tensor_tensor(
-                z[:].rearrange("p (c i t) -> p c t i", i=PACK, t=PACK),
-                step1[:].rearrange("p t (c i) -> p c t i", i=PACK),
-                step2[b][:, :, j0:j1].rearrange("p t (c i) -> p c t i", i=PACK),
+                z[:].rearrange("p (c i t) -> p c t i", i=LINE, t=PACK),
+                diff[:].rearrange("p t (c i) -> p c t i", i=LINE),
+                step2[g][:, :, j0:j1].rearrange("p t (c i) -> p c t i", i=LINE),
                 ALU.max,
             )
             return z
 
-        def project(zq, b, q, z0):
+        def project(zq, g, q, z0):
             codes, scales = zq
             for t in range(PACK):
                 cols = slice(P * t, P * (t + 1))
                 nc.tensor.matmul_mx(
-                    out=y_banks[q][:, t, :], lhsT=w4c[:, b, cols].bitcast(FP8X4), lhsT_scale=w4s[4 * b : P, cols],
+                    out=y_banks[q][:, t, :],
+                    lhsT=w4c[:, g, cols].bitcast(FP8X4), lhsT_scale=w4s[QUAD_BLOCKS * g : P, cols],
                     rhs=codes[:, z0 : z0 + QUARTER].bitcast(FP8X4), rhs_scale=scales[:, z0 : z0 + QUARTER],
-                    start=(b == 0 and t == 0), stop=(b == 1 and t == PACK - 1),
+                    start=(g == 0 and t == 0), stop=(g == GROUPS - 1 and t == PACK - 1),
                 )
 
-        def a_rows(b, t):
-            cols = slice(P * t, P * (t + 1))
-            return first_stage_rows(
-                [(w1q[a, b][0][:, cols].bitcast(FP8X4), w1q[a, b][1][:, cols],
-                  [h.bitcast(FP8X4) for h in halves(v1[a])], halves(s1, 4 * a)) for a in range(2)], 1)
-
-        step1 = in_turn(ring, [P, PACK, J], F32, "raw", 4)
+        step1 = in_turn([P, PACK, J], F32, "raw", RAW_SLOTS)
         for t in range(PACK):
             nc.vector.tensor_tensor(step1[:, t, :], a_rows(0, t)[:].indirect(p1[:]), bt[0][:, t, :], ALU.subtract)
-        w4c = keep.tile([P, 2, N], U32, name="w4c", align_bytes=64)
+        w4c = keep.tile([P, GROUPS, N], U32, name="w4c", align_bytes=64)
         nc.scalar.copy(
-            out=w4c[:].rearrange("p a (t m) -> p a m t", t=PACK),
-            in_=w4_raw[:].rearrange("p a (m t) -> p a m t", t=PACK),
+            out=w4c[:].rearrange("p g (t m) -> p g m t", t=PACK),
+            in_=w4_raw[:].rearrange("p g (m t) -> p g m t", t=PACK),
         )
         w4s = keep.tile([P, N], U8, name="w4s", align_bytes=64)
         nc.vector.tensor_copy(
             out=w4s[:].rearrange("p (t m) -> p m t", t=PACK),
             in_=w4s_raw[:].rearrange("p (m t) -> p m t", t=PACK),
         )
-        z0 = join(step1, 0, 0, J)
+        z_first = join(in_turn([P, PACK * J], BF16, "rounded", ROUNDED_SLOTS), step1, 0, 0, J)
         last_rows = [a_rows(1, t) for t in range(PACK)]
+        zq_first = quantize(z_first[:], "zq0")
+        for q in range(QUARTERS):
+            project(zq_first, 0, q, QUARTER * q)
 
         def finish_z(j0, j1):
-            piece = ring.tile([P, PACK, j1 - j0], F32, name="piece", tag="piece", align_bytes=64)
+            piece = shared([P, PACK, j1 - j0], F32, "piece", "piece")
             for t in range(PACK):
                 nc.vector.tensor_tensor(
-                    piece[:, t, :], last_rows[t][:].indirect(p1[:, j0 // 16 : j1 // 16]),
+                    piece[:, t, :], last_rows[t][:].indirect(p1[:, j0 // LIST_ROWS : j1 // LIST_ROWS]),
                     bt[1][:, t, j0:j1], ALU.subtract)
-            return join(piece, 1, j0, j1)
+            if j1 == J:
+                z = shared([P, PACK * (j1 - j0)], BF16, "z_last", "last_z")
+            else:
+                z = in_turn([P, PACK * (j1 - j0)], BF16, "rounded", ROUNDED_SLOTS)
+            return join(z, piece, 1, j0, j1)
 
         def store_y(q):
-            y = in_turn(ring, [P, PACK, QUARTER], F32, "y", 4)
+            y = in_turn([P, PACK, QUARTER], F32, "y", QUARTERS)
             nc.scalar.copy(out=y[:], in_=y_banks[q][:])
             nc.sync.dma_start(out=out_rows[:, :, QUARTER * q : QUARTER * (q + 1)], in_=y[:])
             return y
@@ -289,10 +308,7 @@ def tile_list_milk_coldstep_features_kernel(
             nc.vector.quantize_mx(out=y_codes[:, j0:j1].bitcast(FP8X4), scales=y_scales[:, j0:j1], in_=y_rounded[:])
             nc.sync.dma_start(out=out_words[:, j0:j1], in_=y_codes[:, j0:j1].bitcast(I32))
 
-        zq0 = quantize(z0[:], "zq0")
-        for q in range(J // QUARTER):
-            project(zq0, 0, q, QUARTER * q)
-        last_q = J // QUARTER - 1
+        last_q = QUARTERS - 1
         y_early = keep.tile([P, PACK * QUARTER * last_q], BF16, name="y_early", align_bytes=64)
         y_last = keep.tile([P, PACK * QUARTER], BF16, name="y_last", align_bytes=64)
         for first, count in PIECES:
@@ -300,22 +316,21 @@ def tile_list_milk_coldstep_features_kernel(
             zq = quantize(z[:], "zq1%d" % first)
             for q in range(first, first + count):
                 project(zq, 1, q, QUARTER * (q - first))
-            for q in range(first, first + count):
-                by_column = y_banks[q][:].rearrange("p t n -> p n t")
-                if q < last_q:
-                    cols = y_early[:, PACK * QUARTER * q : PACK * QUARTER * (q + 1)]
-                    nc.scalar.copy(out=cols.rearrange("p (n t) -> p n t", t=PACK), in_=by_column)
-                    store_y(q)
-        y_codes = ring.tile([P, J], U32, name="y_codes", tag="last_z", align_bytes=64)
+            for q in range(first, min(first + count, last_q)):
+                cols = y_early[:, PACK * QUARTER * q : PACK * QUARTER * (q + 1)]
+                nc.scalar.copy(
+                    out=cols.rearrange("p (n t) -> p n t", t=PACK), in_=y_banks[q][:].rearrange("p t n -> p n t"))
+                store_y(q)
+        y_codes = shared([P, J], U32, "y_codes", "last_z")
         store_codes(y_early, 0, QUARTER * last_q)
         nc.vector.tensor_copy(
-            out=y_last[:].rearrange("p (c i t) -> p c t i", i=PACK, t=PACK),
-            in_=store_y(last_q)[:].rearrange("p t (c i) -> p c t i", i=PACK),
+            out=y_last[:].rearrange("p (c i t) -> p c t i", i=LINE, t=PACK),
+            in_=store_y(last_q)[:].rearrange("p t (c i) -> p c t i", i=LINE),
         )
         store_codes(y_last, QUARTER * last_q, J)
-        for quad in range(4):
+        for quad in range(QUADS):
             queue = nc.scalar if quad % 2 else nc.sync
             queue.dma_start(
-                out=out_2[0, 4 * quad : 4 * quad + 4, :].bitcast(I32),
-                in_=y_scales[32 * quad : 32 * quad + 4, :].bitcast(I32),
+                out=out_2[0, QUAD_BLOCKS * quad : QUAD_BLOCKS * (quad + 1), :].bitcast(I32),
+                in_=y_scales[QUAD * quad : QUAD * quad + QUAD_BLOCKS, :].bitcast(I32),
             )

from contextlib import ExitStack

import concourse.mybir as mybir

K, K2, H, N, T, S, J = 1024, 512, 1024, 512, 4096, 1024, 512
FLOPS = 2 * (K * H * S + 2 * K2 * H * S + H * N * J)

F32 = mybir.dt.float32
BF16 = mybir.dt.bfloat16
I32 = mybir.dt.int32
U32 = mybir.dt.uint32
U16 = mybir.dt.uint16
U8 = mybir.dt.uint8
FP8X4 = mybir.dt.float8_e4m3fn_x4
FP4X4 = mybir.dt.float4_e2m1fn_x4
ALU = mybir.AluOpType
COPY = mybir.ActivationFunctionType.Copy

P = 128
PACK = 4
PASS = P * PACK
A_PASSES = K // PASS
GROUPS = H // PASS
BANK = 512
QUADS, QUAD = 4, 32
BLOCKS = PASS // 32
QUAD_BLOCKS = BLOCKS // QUADS
LIST_ROWS = 16
LINE = 4
QUARTER = BANK // PACK
QUARTERS = J // QUARTER
PIECES = ((0, 2), (2, 1), (3, 1))
RAW_SLOTS, ROUNDED_SLOTS, ROW_SLOTS = 4, 4, GROUPS * PACK


def tile_list_milk_coldstep_features_kernel(
    tc, tab_words, tab_scales, tab2_words, tab2_scales, tab3_words, tab3_scales,
    offs, offs2, offs3, pos1, pos2, pos3, w1, w2_words, w2_scales, w3, w4_words, w4_scales,
    out_0, out_1, out_2,
):
    nc = tc.nc
    with ExitStack() as ctx:
        keep = ctx.enter_context(tc.tile_pool(name="keep", bufs=1))
        ring = ctx.enter_context(tc.tile_pool(name="ring", bufs=1))
        psum = ctx.enter_context(tc.psum_pool(name="psum", bufs=1))

        turns = {}

        def next_turn(kind):
            turns[kind] = turns.get(kind, 0) + 1
            return turns[kind] - 1

        def shared(shape, dtype, name, slot):
            return ring.tile(shape, dtype, name=name, tag=slot, align_bytes=64)

        def in_turn(shape, dtype, kind, slots):
            return shared(shape, dtype, kind, "%s%d" % (kind, next_turn(kind) % slots))

        def load_list(dram, name):
            tile = keep.tile(list(dram.shape), U16, name=name)
            nc.sync.dma_start(tile[:], dram)
            return tile

        def zeroed_bytes(width, name):
            tile = keep.tile([P, width], U8, name=name, align_bytes=64)
            nc.vector.memset(tile[:].bitcast(I32), 0)
            return tile

        def load_plane(plane, scales):
            passes = scales.shape[0]
            for quad in range(QUADS):
                blocks = slice(QUAD_BLOCKS * quad, QUAD_BLOCKS * (quad + 1))
                source = scales[:, blocks, :] if passes > 1 else scales[0, blocks, :]
                nc.sync.dma_start(
                    out=plane[QUAD * quad : QUAD * quad + QUAD_BLOCKS * passes, :].bitcast(I32),
                    in_=source.bitcast(I32),
                )

        def load_spread(window, scales):
            source = scales.rearrange("g b c -> (g b) c")
            nc.sync.dma_start(out=window[0 : P : P // source.shape[0], :].bitcast(I32), in_=source.bitcast(I32))

        def place_rows(plane, picked, passes, kp):
            spacing = P // (BLOCKS * passes)
            for e in range(QUAD_BLOCKS):
                low = spacing * (BLOCKS * kp + e)
                high = low + (QUADS - 1) * QUAD_BLOCKS * spacing
                nc.sync.dma_start(
                    out=plane[QUAD_BLOCKS * kp + e : P : QUAD, :].bitcast(I32),
                    in_=picked[low : high + 1 : QUAD_BLOCKS * spacing, :].bitcast(I32),
                )

        def load_table_words(words, kp, slot):
            tile = shared([P, T], U32, "table", slot)
            nc.sync.dma_start(out=tile[:].bitcast(I32), in_=words[kp].rearrange("p c i -> p (c i)").bitcast(I32))
            return tile

        def load_weight(w, kp, g):
            tile = in_turn([P, PACK, PASS], F32, "raw", RAW_SLOTS)
            nc.sync.dma_start(
                out=tile[:],
                in_=w[PASS * kp : PASS * (kp + 1), PASS * g : PASS * (g + 1)].rearrange("(p i) c -> p i c", i=PACK),
            )
            return tile

        def round_weight(raw):
            rounded = in_turn([P, PACK * PASS], BF16, "rounded", ROUNDED_SLOTS)
            nc.scalar.activation(
                out=rounded[:].rearrange("p (t m i) -> p m i t", t=PACK, i=PACK),
                in_=raw[:].rearrange("p i (m t) -> p m i t", t=PACK),
                func=COPY,
            )
            return rounded

        def quantize(rounded, name, codes=None):
            width = rounded.shape[1] // PACK
            if codes is None:
                codes = keep.tile([P, width], U32, name=name + "_codes", align_bytes=64)[:]
            scales = keep.tile([P, width], U8, name=name + "_scales", align_bytes=64)
            nc.vector.quantize_mx(out=codes.bitcast(FP8X4), scales=scales[:], in_=rounded)
            return codes, scales

        def gather(window, offsets, dtype, name):
            picked = keep.tile([P, LIST_ROWS * offsets.shape[1]], dtype, name=name, align_bytes=64)
            nc.vector.tensor_copy(picked[:], window[:].indirect(offsets))
            return picked

        def halves(tile, first_row=0):
            return [tile[first_row:P, BANK * h : BANK * (h + 1)] for h in range(S // BANK)]

        def slice_rows(operands, negate=False, slot=None):
            turn = next_turn("rows")
            rows = shared([P, S], F32, "rows", slot or "rows%d" % (turn % ROW_SLOTS))
            for half in range(S // BANK):
                bank = psum.tile([P, BANK], F32, name="bank", tag="bank%d" % ((turn + 1) % 2 * 2 + half))
                for kp, (lhsT, lhsT_scale, moving, moving_scale) in enumerate(operands):
                    nc.tensor.matmul_mx(
                        out=bank[:], lhsT=lhsT, lhsT_scale=lhsT_scale, rhs=moving[half], rhs_scale=moving_scale[half],
                        start=(kp == 0), stop=(kp == len(operands) - 1),
                    )
                cols = rows[:, BANK * half : BANK * (half + 1)]
                if negate:
                    nc.scalar.activation(out=cols, in_=bank[:], func=COPY, scale=-1.0)
                else:
                    nc.scalar.copy(out=cols, in_=bank[:])
            return rows

        s2_win = zeroed_bytes(T, "s2_win")
        s3_win = zeroed_bytes(T, "s3_win")
        w2s_raw = zeroed_bytes(H, "w2s_raw")
        s1_win = zeroed_bytes(T, "s1_win")
        w4s_raw = zeroed_bytes(N, "w4s_raw")
        s2, s3, s1 = [zeroed_bytes(S, name) for name in ("s2", "s3", "s1")]

        o2 = load_list(offs2, "o2")
        load_spread(s2_win, tab2_scales)
        o3 = load_list(offs3, "o3")
        load_spread(s3_win, tab3_scales)
        w2_raw = keep.tile([P, H], U16, name="w2_raw")
        nc.sync.dma_start(out=w2_raw[:].bitcast(I32), in_=w2_words[0].bitcast(I32))
        load_plane(w2s_raw, w2_scales)
        w3_raw = [load_weight(w3, 0, 0)]
        t2_win = load_table_words(tab2_words, 0, "big0")
        place_rows(s2, gather(s2_win, o2[:], U8, "s2_picked"), 1, 0)
        o1 = load_list(offs, "o1")
        load_spread(s1_win, tab_scales)
        t3_win = load_table_words(tab3_words, 0, "big1")
        p2 = load_list(pos2, "p2")
        w3_raw.append(load_weight(w3, 0, 1))
        place_rows(s3, gather(s3_win, o3[:], U8, "s3_picked"), 1, 0)
        p3 = load_list(pos3, "p3")
        w1_raw = {(0, 0): load_weight(w1, 0, 0)}
        s1_picked = gather(s1_win, o1[:], U8, "s1_picked")
        place_rows(s1, s1_picked, A_PASSES, 0)
        w1_raw[1, 0] = load_weight(w1, 1, 0)
        place_rows(s1, s1_picked, A_PASSES, 1)
        w1_raw[0, 1] = load_weight(w1, 0, 1)
        t1_win = [load_table_words(tab_words, 0, "big2"), load_table_words(tab_words, 1, "big0")]
        w1_raw[1, 1] = load_weight(w1, 1, 1)
        p1 = load_list(pos1, "p1")
        load_plane(w4s_raw, w4_scales)
        w4_raw = keep.tile([P, GROUPS, N], U32, name="w4_raw")
        nc.sync.dma_start(out=w4_raw[:].bitcast(I32), in_=w4_words.rearrange("g p c i -> p g (c i)").bitcast(I32))

        w2c = keep.tile([P, H], U16, name="w2c", align_bytes=64)
        nc.scalar.copy(
            out=w2c[:].rearrange("p (g t m) -> p g m t", g=GROUPS, t=PACK),
            in_=w2_raw[:].rearrange("p (g m t) -> p g m t", g=GROUPS, t=PACK),
        )
        half_list = BANK // LIST_ROWS
        v2 = [gather(t2_win, o2[:, :half_list], U32, "v2_0")]
        w2s = keep.tile([P, H], U8, name="w2s", align_bytes=64)
        nc.vector.tensor_copy(
            out=w2s[:].rearrange("p (g t m) -> p g m t", g=GROUPS, t=PACK),
            in_=w2s_raw[:].rearrange("p (g m t) -> p g m t", g=GROUPS, t=PACK),
        )
        v2.append(gather(t2_win, o2[:, half_list:], U32, "v2_1"))

        def pick_b(g, picked):
            for t in range(PACK):
                c0 = PASS * g + P * t
                rows = slice_rows([(
                    w2c[:].bitcast(U8)[:, 2 * c0 : 2 * (c0 + P)].bitcast(FP4X4), w2s[:, c0 : c0 + P],
                    [v[:].bitcast(FP8X4) for v in v2], halves(s2))])
                nc.vector.tensor_copy(picked[:, t, :], rows[:].indirect(p2[:]))
            return picked

        bt = [pick_b(0, keep.tile([P, PACK, J], F32, name="bt0"))]
        w3q = [quantize(round_weight(w3_raw[0])[:], "w3q0")]
        v3 = gather(t3_win, o3[:], U32, "v3")
        bt.append(pick_b(1, shared([P, PACK, J], F32, "bt1", "big1")))

        def second_step(g, diff, last_slot=None):
            codes, scales = w3q[g]
            for t in range(PACK):
                cols = slice(P * t, P * (t + 1))
                rows = slice_rows(
                    [(codes[:, cols].bitcast(FP8X4), scales[:, cols],
                      [h.bitcast(FP8X4) for h in halves(v3)], halves(s3))],
                    negate=True, slot=last_slot if t == PACK - 1 else None)
                nc.vector.tensor_tensor(diff[:, t, :], rows[:].indirect(p3[:]), bt[g][:, t, :], ALU.add)
            return diff

        step2 = [second_step(0, keep.tile([P, PACK, J], F32, name="step2_0"))]
        v1 = [gather(t1_win[0], o1[:], U32, "v1_0")]
        codes_mid = shared([P, A_PASSES + 1, PASS], U32, "codes_mid", "big2")
        w3q.append(quantize(round_weight(w3_raw[1])[:], "w3q1", codes_mid[:, A_PASSES, :]))
        w1q = {
            (kp, 0): quantize(round_weight(w1_raw[kp, 0])[:], "w1q%d0" % kp, codes_mid[:, kp, :])
            for kp in range(A_PASSES)
        }
        v1.append(gather(t1_win[1], o1[:], U32, "v1_1"))
        step2.append(second_step(1, shared([P, PACK, J], F32, "step2_1", "big0"), "last_d"))
        codes_late = shared([P, A_PASSES, PASS], U32, "codes_late", "last_d")
        for kp in range(A_PASSES):
            w1q[kp, 1] = quantize(round_weight(w1_raw[kp, 1])[:], "w1q%d1" % kp, codes_late[:, kp, :])

        y_banks = [psum.tile([P, PACK, QUARTER], F32, name="y_bank%d" % q) for q in range(QUARTERS)]
        y_scales = keep.tile([P, J], U8, name="y_scales", align_bytes=64)
        out_rows = out_0.rearrange("(p t) j -> p t j", t=PACK)
        out_words = out_1[0].rearrange("p m t -> p (m t)").bitcast(I32)

        def a_rows(g, t):
            cols = slice(P * t, P * (t + 1))
            return slice_rows(
                [(w1q[kp, g][0][:, cols].bitcast(FP8X4), w1q[kp, g][1][:, cols],
                  [h.bitcast(FP8X4) for h in halves(v1[kp])], halves(s1, QUAD_BLOCKS * kp))
                 for kp in range(A_PASSES)])

        def join(z, diff, g, j0, j1):
            nc.vector.tensor_tensor(
                z[:].rearrange("p (c i t) -> p c t i", i=LINE, t=PACK),
                diff[:].rearrange("p t (c i) -> p c t i", i=LINE),
                step2[g][:, :, j0:j1].rearrange("p t (c i) -> p c t i", i=LINE),
                ALU.max,
            )
            return z

        def project(zq, g, q, z0):
            codes, scales = zq
            for t in range(PACK):
                cols = slice(P * t, P * (t + 1))
                nc.tensor.matmul_mx(
                    out=y_banks[q][:, t, :],
                    lhsT=w4c[:, g, cols].bitcast(FP8X4), lhsT_scale=w4s[QUAD_BLOCKS * g : P, cols],
                    rhs=codes[:, z0 : z0 + QUARTER].bitcast(FP8X4), rhs_scale=scales[:, z0 : z0 + QUARTER],
                    start=(g == 0 and t == 0), stop=(g == GROUPS - 1 and t == PACK - 1),
                )

        step1 = in_turn([P, PACK, J], F32, "raw", RAW_SLOTS)
        for t in range(PACK):
            nc.vector.tensor_tensor(step1[:, t, :], a_rows(0, t)[:].indirect(p1[:]), bt[0][:, t, :], ALU.subtract)
        w4c = keep.tile([P, GROUPS, N], U32, name="w4c", align_bytes=64)
        nc.scalar.copy(
            out=w4c[:].rearrange("p g (t m) -> p g m t", t=PACK),
            in_=w4_raw[:].rearrange("p g (m t) -> p g m t", t=PACK),
        )
        w4s = keep.tile([P, N], U8, name="w4s", align_bytes=64)
        nc.vector.tensor_copy(
            out=w4s[:].rearrange("p (t m) -> p m t", t=PACK),
            in_=w4s_raw[:].rearrange("p (m t) -> p m t", t=PACK),
        )
        z_first = join(in_turn([P, PACK * J], BF16, "rounded", ROUNDED_SLOTS), step1, 0, 0, J)
        last_rows = [a_rows(1, t) for t in range(PACK)]
        zq_first = quantize(z_first[:], "zq0")
        for q in range(QUARTERS):
            project(zq_first, 0, q, QUARTER * q)

        def finish_z(j0, j1):
            piece = shared([P, PACK, j1 - j0], F32, "piece", "piece")
            for t in range(PACK):
                nc.vector.tensor_tensor(
                    piece[:, t, :], last_rows[t][:].indirect(p1[:, j0 // LIST_ROWS : j1 // LIST_ROWS]),
                    bt[1][:, t, j0:j1], ALU.subtract)
            if j1 == J:
                z = shared([P, PACK * (j1 - j0)], BF16, "z_last", "last_z")
            else:
                z = in_turn([P, PACK * (j1 - j0)], BF16, "rounded", ROUNDED_SLOTS)
            return join(z, piece, 1, j0, j1)

        def store_y(q):
            y = in_turn([P, PACK, QUARTER], F32, "y", QUARTERS)
            nc.scalar.copy(out=y[:], in_=y_banks[q][:])
            nc.sync.dma_start(out=out_rows[:, :, QUARTER * q : QUARTER * (q + 1)], in_=y[:])
            return y

        def store_codes(y_rounded, j0, j1):
            nc.vector.quantize_mx(out=y_codes[:, j0:j1].bitcast(FP8X4), scales=y_scales[:, j0:j1], in_=y_rounded[:])
            nc.sync.dma_start(out=out_words[:, j0:j1], in_=y_codes[:, j0:j1].bitcast(I32))

        last_q = QUARTERS - 1
        y_early = keep.tile([P, PACK * QUARTER * last_q], BF16, name="y_early", align_bytes=64)
        y_last = keep.tile([P, PACK * QUARTER], BF16, name="y_last", align_bytes=64)
        for first, count in PIECES:
            z = finish_z(QUARTER * first, QUARTER * (first + count))
            zq = quantize(z[:], "zq1%d" % first)
            for q in range(first, first + count):
                project(zq, 1, q, QUARTER * (q - first))
            for q in range(first, min(first + count, last_q)):
                cols = y_early[:, PACK * QUARTER * q : PACK * QUARTER * (q + 1)]
                nc.scalar.copy(
                    out=cols.rearrange("p (n t) -> p n t", t=PACK), in_=y_banks[q][:].rearrange("p t n -> p n t"))
                store_y(q)
        y_codes = shared([P, J], U32, "y_codes", "last_z")
        store_codes(y_early, 0, QUARTER * last_q)
        nc.vector.tensor_copy(
            out=y_last[:].rearrange("p (c i t) -> p c t i", i=LINE, t=PACK),
            in_=store_y(last_q)[:].rearrange("p t (c i) -> p c t i", i=LINE),
        )
        store_codes(y_last, QUARTER * last_q, J)
        for quad in range(QUADS):
            queue = nc.scalar if quad % 2 else nc.sync
            queue.dma_start(
                out=out_2[0, QUAD_BLOCKS * quad : QUAD_BLOCKS * (quad + 1), :].bitcast(I32),
                in_=y_scales[QUAD * quad : QUAD * quad + QUAD_BLOCKS, :].bitcast(I32),
            )
